import numpy as np, ml_dtypes
CORES = [3,5,19,21,35,37,51,53,67,69]
N = 10
import mx_ref
KO = 4
F = np.float32(0.8)
OWN = [0,0,2,2,0,2,0,2,0,2]
BF = ml_dtypes.bfloat16
def tile(rs):
    return np.stack(rs, axis=2).reshape(128, -1).astype(BF)
def pick(b):
    s = np.zeros((128, 128, 4), np.float32)
    s[np.arange(128), np.arange(128), b] = 1.0
    return mx_ref.quantize(s.reshape(128, 512).astype(BF))
def pk(c, s, i=0):
    return (np.ascontiguousarray(c[:, 512 * i:512 * i + 512]), mx_ref.live(s[:, 128 * i:128 * i + 128]))
def inputs(rng, e, E):
    def f(*shape):
        v = (rng.standard_normal(shape, dtype=np.float32) * np.exp2(rng.integers(-2, 3, shape[:-1] + (1,)))).astype(BF)
        return mx_ref.spread((v.astype(np.float32) * np.exp2(rng.integers(-E, E + 1, shape[:-2] + (1, 1))).astype(np.float32)).astype(BF), rng, e)
    def packed(k):
        c = np.zeros((N, 128, k * 512), np.uint8); s = np.zeros((N, 128, k * 128), np.uint8)
        for r in range(N):
            for i in range(k):
                a, b = mx_ref.quantize(f(128, 512)); c[r][:, 512 * i:512 * i + 512] = a; s[r][:, 128 * i:128 * i + 128] = mx_ref.plane(b, rng)
        return c, s
    d = {}
    d["kc"], d["ks"] = packed(KO)
    d["q"] = f(N, 128, 512)
    return d
def setup_inputs(rng):
    return inputs(rng, 0, 0)
def setup_inputs_blocks(rng):
    return inputs(rng, 4, 0)
def setup_inputs_wide(rng):
    return inputs(rng, 0, 8)
def reference(kc, ks, q):
    S = [pick(t) for t in range(4)]
    anew = lambda p, i: mx_ref.quantize(tile([mx_ref.matmul(S[t], pk(kc[p], ks[p], i)) * F for t in range(4)]))
    y = np.full((N, 128, 2560), np.nan, np.float32)
    for o in range(N):
        if OWN[o] != o: continue
        qq = mx_ref.quantize(q[o])
        M = [pk(kc[o], ks[o], i) for i in range(KO)] + [anew(p, i) for p in range(N) if p != o and OWN[p] == o for i in range(KO)]
        y[o][:, :128 * len(M)] = np.concatenate([mx_ref.matmul(qq, m) for m in M], axis=1)
    return {"y": y}

@@ -1,0 +1,185 @@
+from concourse.bass import DstId, RemoteDMATransfer
+from concourse.mybir import dt, AluOpType, ActivationFunctionType
+
+W = 512
+CUT = 320
+HALF = 256
+LANES = 8
+SCALE = 0.8
+
+SCRATCH = {
+    "diag": ("sbuf", [128, 516], "bfloat16"),
+    "ones": ("sbuf", [128, 128], "bfloat16"),
+    "sc": ("sbuf", [128, 512], "float8_e4m3fn_x4"),
+    "ss": ("sbuf", [128, 512], "uint8"),
+    "xk": ("sbuf", [128, 512], "float8_e4m3fn_x4"),
+    "xp": ("sbuf", [128, 512], "uint8"),
+    "h": ("sbuf", [128, 2048], "bfloat16"),
+    "nk": ("sbuf", [128, 512], "float8_e4m3fn_x4"),
+    "np": ("sbuf", [128, 512], "uint8"),
+    "kk": ("sbuf", [128, 512], "float8_e4m3fn_x4"),
+    "kp": ("sbuf", [128, 512], "uint8"),
+    "qt": ("sbuf", [128, 512], "bfloat16"),
+    "qk": ("sbuf", [128, 128], "float8_e4m3fn_x4"),
+    "qp": ("sbuf", [128, 128], "uint8"),
+    "mk": ("sbuf", [128, 2048], "float8_e4m3fn_x4"),
+    "mp": ("sbuf", [128, 2048], "uint8"),
+    "yo": ("sbuf", [128, 2560], "float32"),
+    "ps": ("psum", [128, 4096], "float32"),
+}
+SEMAPHORES = (["zer", "eye", "sq", "ldp", "ldx", "ldo", "xch", "sent", "ldq", "qq", "outs", "outa"]
+              + ["cast%d" % h for h in range(2)] + ["qz%d" % h for h in range(2)]
+              + ["mm%d" % i for i in range(8)] + ["cp%d" % i for i in range(8)]
+              + ["arr%d_%d" % (s, h) for s in range(4) for h in range(2)])
+
+
+def lanes(topo, src, dst, k):
+    m, out = topo.mask(src, dst), 0
+    for _ in range(k):
+        low = m & -m
+        out |= low
+        m ^= low
+    return out
+
+
+def producers(T, o):
+    own = T.tables["OWN"]
+    return [p for p in range(len(own)) if own[p] == o and p != o]
+
+
+def neighbour(T, topo, p):
+    own, c = T.tables["OWN"], T.cores
+    here = topo.chip(c[p])
+    for r in range(len(own)):
+        if (r != p and own[r] != r and own[p] != p and own[r] != own[p] and topo.chip(c[r]) == here
+                and topo.die(c[r]) != topo.die(c[p])
+                and topo.chip(c[own[r]]) != here and topo.chip(c[own[p]]) != here):
+            return r
+    return None
+
+
+def cut(T, topo, p):
+    return HALF if neighbour(T, topo, p) is None else CUT
+
+
+def produce(g, core, T, topo, rank):
+    own = T.tables["OWN"]
+    S = T.sem
+    other = neighbour(T, topo, rank)
+    c = cut(T, topo, rank)
+
+    g.scalar.dma_start(T.kp[:, 0:W], T.ks[:, 0:W]).then_inc(S.ldp, 16)
+
+    def load(a, b, sem):
+        g.sync.dma_start(T.kk[:, a:b].bitcast(dt.uint8), T.kc[:, 4 * a:4 * b]).then_inc(sem, 16)
+    if other is not None:
+        load(c, W, S.ldx)
+        load(0, c, S.ldo)
+    else:
+        load(0, c, S.ldo)
+        load(c, W, S.ldx)
+
+    g.vector.memset(T.ones[:], 1.0).then_inc(S.zer, 1)
+    g.vector.memset(T.diag[:], 0.0).then_inc(S.zer, 1)
+    g.wait_ge(S.zer, 2)
+    g.affine_select(T.diag[:, 3:515:4], T.ones[:], [[-1, 128]], AluOpType.is_equal, 0.0, 0, 1).then_inc(S.eye, 1)
+    g.vector.wait_ge(S.eye, 1)
+    for b in range(4):
+        g.vector.quantize_mx(T.sc[:, 128 * b:128 * b + 128], T.ss[:, 128 * b:128 * b + 128],
+                             T.diag[:, 3 - b:515 - b]).then_inc(S.sq, 1)
+
+    sent = [0]
+
+    def write(dst, out, in_, sem):
+        rid, pid, _ = topo.addr(dst)
+        g.remote_dma(out, in_, sem, S.sent, pid, rid, lanes(topo, core, dst, LANES))
+        sent[0] += LANES
+
+    if other is not None:
+        g.wait_ge(S.ldp, 16)
+        write(T.cores[other], T.xp[:, 0:W - c], T.kp[:, c:W], S.xch)
+        g.wait_ge(S.ldx, 16)
+        write(T.cores[other], T.xk[:, 0:W - c].bitcast(dt.uint8), T.kk[:, c:W].bitcast(dt.uint8), S.xch)
+
+    parts = [(T.kk, T.kp, 0, c, 0, rank, [(S.ldp, 16), (S.ldo, 16)])]
+    if other is not None:
+        parts.append((T.xk, T.xp, 0, W - c, c, other, [(S.xch, 2 * LANES)]))
+    else:
+        parts.append((T.kk, T.kp, c, W - c, c, rank, [(S.ldx, 16)]))
+    g.tensor.wait_ge(S.sq, 4)
+    for h, (codes, planes, a, n, d, who, waits) in enumerate(parts):
+        for sem, val in waits:
+            g.tensor.wait_ge(sem, val)
+        for b in range(4):
+            bank = 512 * (4 * h + b)
+            out = T.ps[:, bank:bank + n]
+            done = S["mm%d" % (4 * h + b)]
+            g.tensor.matmul_mx(out, T.sc[:, 128 * b:128 * b + 128], T.ss[:, 128 * b:128 * b + 128],
+                               codes[:, a:a + n], planes[:, a:a + n], True, True).then_inc(done, 1)
+            to = T.h[:, 4 * d + b:4 * (d + n):4]
+            if b % 2 == 0:
+                g.vector.wait_ge(done, 1)
+                g.vector.tensor_scalar(to, out, SCALE, None, AluOpType.mult).then_inc(S["cast%d" % h], 1)
+            else:
+                g.scalar.wait_ge(done, 1)
+                g.scalar.activation(to, out, ActivationFunctionType.Copy, scale=SCALE).then_inc(S["cast%d" % h], 1)
+        g.vector.wait_ge(S["cast%d" % h], 4)
+        g.vector.quantize_mx(T.nk[:, d:d + n], T.np[:, d:d + n], T.h[:, 4 * d:4 * (d + n)]).then_inc(S["qz%d" % h], 1)
+        o = own[who]
+        slot = producers(T, o).index(who)
+        to, sem = 512 * slot + d, S["arr%d_%d" % (slot, h)]
+        g.wait_ge(S["qz%d" % h], 1)
+        write(T.cores[o], T.mk[:, to:to + n].bitcast(dt.uint8), T.nk[:, d:d + n].bitcast(dt.uint8), sem)
+        write(T.cores[o], T.mp[:, to:to + n], T.np[:, d:d + n], sem)
+    g.wait_ge(S.sent, sent[0])
+
+
+def consume(g, core, T, topo, rank):
+    S = T.sem
+    g.sync.dma_start(T.qt[:], T.q[:, 0:512]).then_inc(S.ldq, 16)
+    g.scalar.dma_start(T.kp[:], T.ks[:, 0:W]).then_inc(S.ldp, 16)
+    g.sync.dma_start(T.kk[:].bitcast(dt.uint8), T.kc[:, 0:4 * W]).then_inc(S.ldo, 16)
+    g.vector.wait_ge(S.ldq, 16)
+    g.vector.quantize_mx(T.qk[:], T.qp[:], T.qt[:]).then_inc(S.qq, 1)
+
+    mine = [(T.kk, T.kp, 0, W, 0, [(S.qq, 1), (S.ldp, 16), (S.ldo, 16)])]
+    first, near, second = [], [], []
+    for s, p in enumerate(producers(T, rank)):
+        c = cut(T, topo, p)
+        arr = [(S["arr%d_%d" % (s, h)], 2 * LANES) for h in range(2)]
+        if neighbour(T, topo, p) is None:
+            near.append((T.mk, T.mp, 512 * s, W, W + 512 * s, arr))
+        else:
+            first.append((T.mk, T.mp, 512 * s, c, W + 512 * s, arr[:1]))
+            second.append((T.mk, T.mp, 512 * s + c, W - c, W + 512 * s + c, arr[1:]))
+    n_sync = n_act = 0
+    for i, (codes, planes, a, n, d, waits) in enumerate(mine + first + near + second):
+        for sem, val in waits:
+            g.tensor.wait_ge(sem, val)
+        out = T.ps[:, 512 * i:512 * i + n]
+        g.tensor.matmul_mx(out, T.qk[:], T.qp[:], codes[:, a:a + n], planes[:, a:a + n], True, True).then_inc(S["mm%d" % i], 1)
+        done = S["cp%d" % i]
+        if i % 2 == 0:
+            g.vector.wait_ge(S["mm%d" % i], 1)
+            g.vector.tensor_copy(T.yo[:, d:d + n], out).then_inc(done, 1)
+            g.sync.wait_ge(done, 1)
+            g.sync.dma_start(T.y[:, d:d + n], T.yo[:, d:d + n]).then_inc(S.outs, 16)
+            n_sync += 16
+        else:
+            g.scalar.wait_ge(S["mm%d" % i], 1)
+            g.scalar.activation(T.yo[:, d:d + n], out, ActivationFunctionType.Copy).then_inc(done, 1)
+            g.scalar.wait_ge(done, 1)
+            g.scalar.dma_start(T.y[:, d:d + n], T.yo[:, d:d + n]).then_inc(S.outa, 16)
+            n_act += 16
+    g.sync.wait_ge(S.outs, n_sync)
+    g.scalar.wait_ge(S.outa, n_act)
+
+
+def rank_program(g, core, T, topo):
+    rank = T.rank_of(core)
+    if rank is None:
+        return
+    if T.tables["OWN"][rank] == rank:
+        consume(g, core, T, topo, rank)
+    else:
+        produce(g, core, T, topo, rank)

@@ -1,10 +1,9 @@
-from concourse.bass import DstId, RemoteDMATransfer
 from concourse.mybir import dt, AluOpType, ActivationFunctionType
 
 W = 512
-CUT = 320
-HALF = 256
-LANES = 8
+CUT = 272
+NEAR = 128
+FAR_K, NEAR_K = 4, 8
 SCALE = 0.8
 
 SCRATCH = {
@@ -33,13 +32,12 @@ SEMAPHORES = (["zer", "eye", "sq", "ldp", "ldx", "ldo", "xch", "sent", "ldq", "q
               + ["arr%d_%d" % (s, h) for s in range(4) for h in range(2)])
 
 
-def lanes(topo, src, dst, k):
-    m, out = topo.mask(src, dst), 0
-    for _ in range(k):
-        low = m & -m
-        out |= low
-        m ^= low
-    return out
+def lanes(topo, src, dst, pick):
+    m, bits = topo.mask(src, dst), []
+    while m:
+        bits.append(m & -m)
+        m &= m - 1
+    return sum(bits[pick]), len(bits[pick])
 
 
 def producers(T, o):
@@ -58,21 +56,18 @@ def neighbour(T, topo, p):
     return None
 
 
-def cut(T, topo, p):
-    return HALF if neighbour(T, topo, p) is None else CUT
-
-
 def produce(g, core, T, topo, rank):
     own = T.tables["OWN"]
     S = T.sem
     other = neighbour(T, topo, rank)
-    c = cut(T, topo, rank)
+    swap = other is not None
+    c = CUT if swap else NEAR
 
     g.scalar.dma_start(T.kp[:, 0:W], T.ks[:, 0:W]).then_inc(S.ldp, 16)
 
     def load(a, b, sem):
         g.sync.dma_start(T.kk[:, a:b].bitcast(dt.uint8), T.kc[:, 4 * a:4 * b]).then_inc(sem, 16)
-    if other is not None:
+    if swap:
         load(c, W, S.ldx)
         load(0, c, S.ldo)
     else:
@@ -90,20 +85,28 @@ def produce(g, core, T, topo, rank):
 
     sent = [0]
 
-    def write(dst, out, in_, sem):
+    def write(dst, out, in_, sem, pick):
         rid, pid, _ = topo.addr(dst)
-        g.remote_dma(out, in_, sem, S.sent, pid, rid, lanes(topo, core, dst, LANES))
-        sent[0] += LANES
+        mask, k = lanes(topo, core, dst, pick)
+        g.remote_dma(out, in_, sem, S.sent, pid, rid, mask)
+        sent[0] += k
 
-    if other is not None:
-        g.wait_ge(S.ldp, 16)
-        write(T.cores[other], T.xp[:, 0:W - c], T.kp[:, c:W], S.xch)
+    def write_codes(dst, to, a, n, sem, pick):
+        write(dst, T.mk[:, to:to + n].bitcast(dt.uint8), T.nk[:, a:a + n].bitcast(dt.uint8), sem, pick)
+
+    def write_planes(dst, to, a, n, sem, pick):
+        write(dst, T.mp[:, to:to + n], T.np[:, a:a + n], sem, pick)
+
+    if swap:
         g.wait_ge(S.ldx, 16)
-        write(T.cores[other], T.xk[:, 0:W - c].bitcast(dt.uint8), T.kk[:, c:W].bitcast(dt.uint8), S.xch)
+        write(T.cores[other], T.xk[:, 0:W - c].bitcast(dt.uint8), T.kk[:, c:W].bitcast(dt.uint8), S.xch,
+              slice(0, 2 * FAR_K, 2))
+        g.wait_ge(S.ldp, 16)
+        write(T.cores[other], T.xp[:, 0:W - c], T.kp[:, c:W], S.xch, slice(1, 2 * FAR_K, 2))
 
     parts = [(T.kk, T.kp, 0, c, 0, rank, [(S.ldp, 16), (S.ldo, 16)])]
-    if other is not None:
-        parts.append((T.xk, T.xp, 0, W - c, c, other, [(S.xch, 2 * LANES)]))
+    if swap:
+        parts.append((T.xk, T.xp, 0, W - c, c, other, [(S.xch, 2 * FAR_K)]))
     else:
         parts.append((T.kk, T.kp, c, W - c, c, rank, [(S.ldx, 16)]))
     g.tensor.wait_ge(S.sq, 4)
@@ -127,10 +130,17 @@ def produce(g, core, T, topo, rank):
         g.vector.quantize_mx(T.nk[:, d:d + n], T.np[:, d:d + n], T.h[:, 4 * d:4 * (d + n)]).then_inc(S["qz%d" % h], 1)
         o = own[who]
         slot = producers(T, o).index(who)
-        to, sem = 512 * slot + d, S["arr%d_%d" % (slot, h)]
+        to = 512 * slot + d
         g.wait_ge(S["qz%d" % h], 1)
-        write(T.cores[o], T.mk[:, to:to + n].bitcast(dt.uint8), T.nk[:, d:d + n].bitcast(dt.uint8), sem)
-        write(T.cores[o], T.mp[:, to:to + n], T.np[:, d:d + n], sem)
+        if swap:
+            pick = slice(FAR_K * h, FAR_K * h + FAR_K)
+            write_codes(T.cores[o], to, d, n, S["arr%d_%d" % (slot, h)], pick)
+            write_planes(T.cores[o], to, d, n, S["arr%d_%d" % (slot, h)], pick)
+        else:
+            pick = slice(0, NEAR_K)
+            write_codes(T.cores[o], to, d, n, S["arr%d_0" % slot], pick)
+            if h == 1:
+                write_planes(T.cores[o], 512 * slot, 0, W, S["arr%d_0" % slot], pick)
     g.wait_ge(S.sent, sent[0])
 
 
@@ -145,15 +155,13 @@ def consume(g, core, T, topo, rank):
     mine = [(T.kk, T.kp, 0, W, 0, [(S.qq, 1), (S.ldp, 16), (S.ldo, 16)])]
     first, near, second = [], [], []
     for s, p in enumerate(producers(T, rank)):
-        c = cut(T, topo, p)
-        arr = [(S["arr%d_%d" % (s, h)], 2 * LANES) for h in range(2)]
         if neighbour(T, topo, p) is None:
-            near.append((T.mk, T.mp, 512 * s, W, W + 512 * s, arr))
+            near.append((T.mk, T.mp, 512 * s, W, W + 512 * s, [(S["arr%d_0" % s], 3 * NEAR_K)]))
         else:
-            first.append((T.mk, T.mp, 512 * s, c, W + 512 * s, arr[:1]))
-            second.append((T.mk, T.mp, 512 * s + c, W - c, W + 512 * s + c, arr[1:]))
+            first.append((T.mk, T.mp, 512 * s, CUT, W + 512 * s, [(S["arr%d_0" % s], 2 * FAR_K)]))
+            second.append((T.mk, T.mp, 512 * s + CUT, W - CUT, W + 512 * s + CUT, [(S["arr%d_1" % s], 2 * FAR_K)]))
     n_sync = n_act = 0
-    for i, (codes, planes, a, n, d, waits) in enumerate(mine + first + near + second):
+    for i, (codes, planes, a, n, d, waits) in enumerate(mine + near + first + second):
         for sem, val in waits:
             g.tensor.wait_ge(sem, val)
         out = T.ps[:, 512 * i:512 * i + n]

@@ -1,10 +1,14 @@
 from concourse.mybir import dt, AluOpType, ActivationFunctionType
 
 W = 512
-CUT = 272
-NEAR = 128
-FAR_K, NEAR_K = 4, 8
+SWAPS = (240, 224, 208)
+KEPT = 128
+NEAR = (128, 192, 192)
 SCALE = 0.8
+XCH_E = slice(0, 8, 1)
+KEPT_E = slice(0, 8, 2)
+SWAP_E = slice(1, 8, 2)
+NEAR_E = slice(0, 16, 1)
 
 SCRATCH = {
     "diag": ("sbuf", [128, 516], "bfloat16"),
@@ -26,18 +30,23 @@ SCRATCH = {
     "yo": ("sbuf", [128, 2560], "float32"),
     "ps": ("psum", [128, 4096], "float32"),
 }
-SEMAPHORES = (["zer", "eye", "sq", "ldp", "ldx", "ldo", "xch", "sent", "ldq", "qq", "outs", "outa"]
-              + ["cast%d" % h for h in range(2)] + ["qz%d" % h for h in range(2)]
-              + ["mm%d" % i for i in range(8)] + ["cp%d" % i for i in range(8)]
-              + ["arr%d_%d" % (s, h) for s in range(4) for h in range(2)])
+SEMAPHORES = (["zer", "eye", "ldp", "ldpx", "ldx", "ldo", "xch", "sent", "ldq", "qq", "outs", "outa"]
+              + ["sq%d" % b for b in range(4)]
+              + ["cast%d" % h for h in range(3)] + ["qz%d" % h for h in range(3)]
+              + ["mm%d" % i for i in range(12)] + ["cp%d" % i for i in range(12)]
+              + ["arr%d_%d" % (s, h) for s in range(4) for h in range(3)])
 
 
-def lanes(topo, src, dst, pick):
+def engines(topo, src, dst, pick):
     m, bits = topo.mask(src, dst), []
     while m:
         bits.append(m & -m)
         m &= m - 1
     return sum(bits[pick]), len(bits[pick])
+
+
+def count(pick):
+    return len(range(pick.start, pick.stop, pick.step))
 
 
 def producers(T, o):
@@ -56,91 +65,101 @@ def neighbour(T, topo, p):
     return None
 
 
+def swaps(T, topo, p):
+    far = sorted({topo.chip(T.cores[r]) for r in range(len(T.cores)) if neighbour(T, topo, r) is not None})
+    return SWAPS[far.index(topo.chip(T.cores[p])) % len(SWAPS)]
+
+
+def near_pieces():
+    return [(sum(NEAR[:h]), n) for h, n in enumerate(NEAR)]
+
+
 def produce(g, core, T, topo, rank):
     own = T.tables["OWN"]
     S = T.sem
     other = neighbour(T, topo, rank)
     swap = other is not None
-    c = CUT if swap else NEAR
+    cut = W - swaps(T, topo, rank) if swap else NEAR[0]
 
-    g.scalar.dma_start(T.kp[:, 0:W], T.ks[:, 0:W]).then_inc(S.ldp, 16)
-
-    def load(a, b, sem):
+    def load_codes(a, b, sem):
         g.sync.dma_start(T.kk[:, a:b].bitcast(dt.uint8), T.kc[:, 4 * a:4 * b]).then_inc(sem, 16)
+
+    def load_planes(a, b, sem):
+        g.scalar.dma_start(T.kp[:, a:b], T.ks[:, a:b]).then_inc(sem, 16)
+
     if swap:
-        load(c, W, S.ldx)
-        load(0, c, S.ldo)
+        load_planes(cut, W, S.ldpx)
+        load_codes(cut, W, S.ldx)
+        load_planes(0, cut, S.ldp)
+        load_codes(0, cut, S.ldo)
     else:
-        load(0, c, S.ldo)
-        load(c, W, S.ldx)
+        load_planes(0, W, S.ldp)
+        load_codes(0, cut, S.ldo)
+        load_codes(cut, W, S.ldx)
 
     g.vector.memset(T.ones[:], 1.0).then_inc(S.zer, 1)
-    g.vector.memset(T.diag[:], 0.0).then_inc(S.zer, 1)
-    g.wait_ge(S.zer, 2)
+    for b in range(3):
+        g.vector.memset(T.diag[:, b:516:4], 0.0).then_inc(S.eye, 1)
+    g.wait_ge(S.zer, 1)
     g.affine_select(T.diag[:, 3:515:4], T.ones[:], [[-1, 128]], AluOpType.is_equal, 0.0, 0, 1).then_inc(S.eye, 1)
-    g.vector.wait_ge(S.eye, 1)
+    g.vector.wait_ge(S.eye, 4)
     for b in range(4):
         g.vector.quantize_mx(T.sc[:, 128 * b:128 * b + 128], T.ss[:, 128 * b:128 * b + 128],
-                             T.diag[:, 3 - b:515 - b]).then_inc(S.sq, 1)
+                             T.diag[:, 3 - b:515 - b]).then_inc(S["sq%d" % b], 1)
 
     sent = [0]
 
     def write(dst, out, in_, sem, pick):
         rid, pid, _ = topo.addr(dst)
-        mask, k = lanes(topo, core, dst, pick)
+        mask, k = engines(topo, core, dst, pick)
         g.remote_dma(out, in_, sem, S.sent, pid, rid, mask)
         sent[0] += k
 
-    def write_codes(dst, to, a, n, sem, pick):
-        write(dst, T.mk[:, to:to + n].bitcast(dt.uint8), T.nk[:, a:a + n].bitcast(dt.uint8), sem, pick)
-
-    def write_planes(dst, to, a, n, sem, pick):
-        write(dst, T.mp[:, to:to + n], T.np[:, a:a + n], sem, pick)
-
     if swap:
+        g.wait_ge(S.ldpx, 16)
+        write(T.cores[other], T.xp[:, cut:W], T.kp[:, cut:W], S.xch, XCH_E)
         g.wait_ge(S.ldx, 16)
-        write(T.cores[other], T.xk[:, 0:W - c].bitcast(dt.uint8), T.kk[:, c:W].bitcast(dt.uint8), S.xch,
-              slice(0, 2 * FAR_K, 2))
-        g.wait_ge(S.ldp, 16)
-        write(T.cores[other], T.xp[:, 0:W - c], T.kp[:, c:W], S.xch, slice(1, 2 * FAR_K, 2))
+        write(T.cores[other], T.xk[:, cut:W].bitcast(dt.uint8), T.kk[:, cut:W].bitcast(dt.uint8), S.xch, XCH_E)
 
-    parts = [(T.kk, T.kp, 0, c, 0, rank, [(S.ldp, 16), (S.ldo, 16)])]
+    mine = [(S.ldp, 16), (S.ldo, 16)]
     if swap:
-        parts.append((T.xk, T.xp, 0, W - c, c, other, [(S.xch, 2 * FAR_K)]))
+        parts = [(T.kk, T.kp, 0, KEPT, rank, mine, KEPT_E, None, 0),
+                 (T.kk, T.kp, KEPT, cut - KEPT, rank, [], KEPT_E, (0, cut), 0),
+                 (T.xk, T.xp, cut, W - cut, other, [(S.xch, 2 * count(XCH_E))], SWAP_E, (cut, W - cut), 1)]
     else:
-        parts.append((T.kk, T.kp, c, W - c, c, rank, [(S.ldx, 16)]))
-    g.tensor.wait_ge(S.sq, 4)
-    for h, (codes, planes, a, n, d, who, waits) in enumerate(parts):
+        parts = [(T.kk, T.kp, a, n, rank, [mine, [(S.ldx, 16)], []][h], NEAR_E, (a, n), h)
+                 for h, (a, n) in enumerate(near_pieces())]
+    for h, (codes, planes, a, n, who, waits, pick, after, part) in enumerate(parts):
         for sem, val in waits:
             g.tensor.wait_ge(sem, val)
+        if h >= 2:
+            g.tensor.wait_ge(S["cast%d" % (h - 2)], 4)
         for b in range(4):
-            bank = 512 * (4 * h + b)
+            if h == 0:
+                g.tensor.wait_ge(S["sq%d" % b], 1)
+            bank = 512 * (4 * (h % 2) + b)
             out = T.ps[:, bank:bank + n]
             done = S["mm%d" % (4 * h + b)]
             g.tensor.matmul_mx(out, T.sc[:, 128 * b:128 * b + 128], T.ss[:, 128 * b:128 * b + 128],
                                codes[:, a:a + n], planes[:, a:a + n], True, True).then_inc(done, 1)
-            to = T.h[:, 4 * d + b:4 * (d + n):4]
-            if b % 2 == 0:
+            to = T.h[:, 4 * a + b:4 * (a + n):4]
+            if b % 2 == 1:
                 g.vector.wait_ge(done, 1)
                 g.vector.tensor_scalar(to, out, SCALE, None, AluOpType.mult).then_inc(S["cast%d" % h], 1)
             else:
                 g.scalar.wait_ge(done, 1)
                 g.scalar.activation(to, out, ActivationFunctionType.Copy, scale=SCALE).then_inc(S["cast%d" % h], 1)
         g.vector.wait_ge(S["cast%d" % h], 4)
-        g.vector.quantize_mx(T.nk[:, d:d + n], T.np[:, d:d + n], T.h[:, 4 * d:4 * (d + n)]).then_inc(S["qz%d" % h], 1)
+        g.vector.quantize_mx(T.nk[:, a:a + n], T.np[:, a:a + n], T.h[:, 4 * a:4 * (a + n)]).then_inc(S["qz%d" % h], 1)
         o = own[who]
         slot = producers(T, o).index(who)
-        to = 512 * slot + d
+        sem = S["arr%d_%d" % (slot, part)]
+        to = 512 * slot
         g.wait_ge(S["qz%d" % h], 1)
-        if swap:
-            pick = slice(FAR_K * h, FAR_K * h + FAR_K)
-            write_codes(T.cores[o], to, d, n, S["arr%d_%d" % (slot, h)], pick)
-            write_planes(T.cores[o], to, d, n, S["arr%d_%d" % (slot, h)], pick)
-        else:
-            pick = slice(0, NEAR_K)
-            write_codes(T.cores[o], to, d, n, S["arr%d_0" % slot], pick)
-            if h == 1:
-                write_planes(T.cores[o], 512 * slot, 0, W, S["arr%d_0" % slot], pick)
+        write(T.cores[o], T.mk[:, to + a:to + a + n].bitcast(dt.uint8), T.nk[:, a:a + n].bitcast(dt.uint8), sem, pick)
+        if after:
+            d, m = after
+            write(T.cores[o], T.mp[:, to + d:to + d + m], T.np[:, d:d + m], sem, pick)
     g.wait_ge(S.sent, sent[0])
 
 
@@ -156,18 +175,27 @@ def consume(g, core, T, topo, rank):
     first, near, second = [], [], []
     for s, p in enumerate(producers(T, rank)):
         if neighbour(T, topo, p) is None:
-            near.append((T.mk, T.mp, 512 * s, W, W + 512 * s, [(S["arr%d_0" % s], 3 * NEAR_K)]))
+            for h, (a, n) in enumerate(near_pieces()):
+                near.append((T.mk, T.mp, 512 * s + a, n, W + 512 * s + a, [(S["arr%d_%d" % (s, h)], 2 * count(NEAR_E))]))
         else:
-            first.append((T.mk, T.mp, 512 * s, CUT, W + 512 * s, [(S["arr%d_0" % s], 2 * FAR_K)]))
-            second.append((T.mk, T.mp, 512 * s + CUT, W - CUT, W + 512 * s + CUT, [(S["arr%d_1" % s], 2 * FAR_K)]))
+            x = swaps(T, topo, p)
+            c = W - x
+            first.append((T.mk, T.mp, 512 * s, c, W + 512 * s, [(S["arr%d_0" % s], 3 * count(KEPT_E))]))
+            second.append((T.mk, T.mp, 512 * s + c, x, W + 512 * s + c, [(S["arr%d_1" % s], 2 * count(SWAP_E))]))
+    first.sort(key=lambda e: e[3])
+    second.sort(key=lambda e: e[3])
+    chunks = mine + near + first + second
     n_sync = n_act = 0
-    for i, (codes, planes, a, n, d, waits) in enumerate(mine + near + first + second):
+    for i, (codes, planes, a, n, d, waits) in enumerate(chunks):
         for sem, val in waits:
             g.tensor.wait_ge(sem, val)
-        out = T.ps[:, 512 * i:512 * i + n]
+        if i >= 8:
+            g.tensor.wait_ge(S["cp%d" % (i - 8)], 1)
+        bank = 512 * (i % 8)
+        out = T.ps[:, bank:bank + n]
         g.tensor.matmul_mx(out, T.qk[:], T.qp[:], codes[:, a:a + n], planes[:, a:a + n], True, True).then_inc(S["mm%d" % i], 1)
         done = S["cp%d" % i]
-        if i % 2 == 0:
+        if (len(chunks) - i) % 2 == 1:
             g.vector.wait_ge(S["mm%d" % i], 1)
             g.vector.tensor_copy(T.yo[:, d:d + n], out).then_inc(done, 1)
             g.sync.wait_ge(done, 1)

from concourse.mybir import dt, AluOpType, ActivationFunctionType

W = 512
SWAPS = (240, 224, 208)
KEPT = 128
NEAR = (128, 192, 192)
SCALE = 0.8
XCH_E = slice(0, 8, 1)
KEPT_E = slice(0, 8, 2)
SWAP_E = slice(1, 8, 2)
NEAR_E = slice(0, 16, 1)

SCRATCH = {
    "diag": ("sbuf", [128, 516], "bfloat16"),
    "ones": ("sbuf", [128, 128], "bfloat16"),
    "sc": ("sbuf", [128, 512], "float8_e4m3fn_x4"),
    "ss": ("sbuf", [128, 512], "uint8"),
    "xk": ("sbuf", [128, 512], "float8_e4m3fn_x4"),
    "xp": ("sbuf", [128, 512], "uint8"),
    "h": ("sbuf", [128, 2048], "bfloat16"),
    "nk": ("sbuf", [128, 512], "float8_e4m3fn_x4"),
    "np": ("sbuf", [128, 512], "uint8"),
    "kk": ("sbuf", [128, 512], "float8_e4m3fn_x4"),
    "kp": ("sbuf", [128, 512], "uint8"),
    "qt": ("sbuf", [128, 512], "bfloat16"),
    "qk": ("sbuf", [128, 128], "float8_e4m3fn_x4"),
    "qp": ("sbuf", [128, 128], "uint8"),
    "mk": ("sbuf", [128, 2048], "float8_e4m3fn_x4"),
    "mp": ("sbuf", [128, 2048], "uint8"),
    "yo": ("sbuf", [128, 2560], "float32"),
    "ps": ("psum", [128, 4096], "float32"),
}
SEMAPHORES = (["zer", "eye", "ldp", "ldpx", "ldx", "ldo", "xch", "sent", "ldq", "qq", "outs", "outa"]
              + ["sq%d" % b for b in range(4)]
              + ["cast%d" % h for h in range(3)] + ["qz%d" % h for h in range(3)]
              + ["mm%d" % i for i in range(12)] + ["cp%d" % i for i in range(12)]
              + ["arr%d_%d" % (s, h) for s in range(4) for h in range(3)])


def engines(topo, src, dst, pick):
    m, bits = topo.mask(src, dst), []
    while m:
        bits.append(m & -m)
        m &= m - 1
    return sum(bits[pick]), len(bits[pick])


def count(pick):
    return len(range(pick.start, pick.stop, pick.step))


def producers(T, o):
    own = T.tables["OWN"]
    return [p for p in range(len(own)) if own[p] == o and p != o]


def neighbour(T, topo, p):
    own, c = T.tables["OWN"], T.cores
    here = topo.chip(c[p])
    for r in range(len(own)):
        if (r != p and own[r] != r and own[p] != p and own[r] != own[p] and topo.chip(c[r]) == here
                and topo.die(c[r]) != topo.die(c[p])
                and topo.chip(c[own[r]]) != here and topo.chip(c[own[p]]) != here):
            return r
    return None


def swaps(T, topo, p):
    far = sorted({topo.chip(T.cores[r]) for r in range(len(T.cores)) if neighbour(T, topo, r) is not None})
    return SWAPS[far.index(topo.chip(T.cores[p])) % len(SWAPS)]


def near_pieces():
    return [(sum(NEAR[:h]), n) for h, n in enumerate(NEAR)]


def produce(g, core, T, topo, rank):
    own = T.tables["OWN"]
    S = T.sem
    other = neighbour(T, topo, rank)
    swap = other is not None
    cut = W - swaps(T, topo, rank) if swap else NEAR[0]

    def load_codes(a, b, sem):
        g.sync.dma_start(T.kk[:, a:b].bitcast(dt.uint8), T.kc[:, 4 * a:4 * b]).then_inc(sem, 16)

    def load_planes(a, b, sem):
        g.scalar.dma_start(T.kp[:, a:b], T.ks[:, a:b]).then_inc(sem, 16)

    if swap:
        load_planes(cut, W, S.ldpx)
        load_codes(cut, W, S.ldx)
        load_planes(0, cut, S.ldp)
        load_codes(0, cut, S.ldo)
    else:
        load_planes(0, W, S.ldp)
        load_codes(0, cut, S.ldo)
        load_codes(cut, W, S.ldx)

    g.vector.memset(T.ones[:], 1.0).then_inc(S.zer, 1)
    for b in range(3):
        g.vector.memset(T.diag[:, b:516:4], 0.0).then_inc(S.eye, 1)
    g.wait_ge(S.zer, 1)
    g.affine_select(T.diag[:, 3:515:4], T.ones[:], [[-1, 128]], AluOpType.is_equal, 0.0, 0, 1).then_inc(S.eye, 1)
    g.vector.wait_ge(S.eye, 4)
    for b in range(4):
        g.vector.quantize_mx(T.sc[:, 128 * b:128 * b + 128], T.ss[:, 128 * b:128 * b + 128],
                             T.diag[:, 3 - b:515 - b]).then_inc(S["sq%d" % b], 1)

    sent = [0]

    def write(dst, out, in_, sem, pick):
        rid, pid, _ = topo.addr(dst)
        mask, k = engines(topo, core, dst, pick)
        g.remote_dma(out, in_, sem, S.sent, pid, rid, mask)
        sent[0] += k

    if swap:
        g.wait_ge(S.ldpx, 16)
        write(T.cores[other], T.xp[:, cut:W], T.kp[:, cut:W], S.xch, XCH_E)
        g.wait_ge(S.ldx, 16)
        write(T.cores[other], T.xk[:, cut:W].bitcast(dt.uint8), T.kk[:, cut:W].bitcast(dt.uint8), S.xch, XCH_E)

    mine = [(S.ldp, 16), (S.ldo, 16)]
    if swap:
        parts = [(T.kk, T.kp, 0, KEPT, rank, mine, KEPT_E, None, 0),
                 (T.kk, T.kp, KEPT, cut - KEPT, rank, [], KEPT_E, (0, cut), 0),
                 (T.xk, T.xp, cut, W - cut, other, [(S.xch, 2 * count(XCH_E))], SWAP_E, (cut, W - cut), 1)]
    else:
        parts = [(T.kk, T.kp, a, n, rank, [mine, [(S.ldx, 16)], []][h], NEAR_E, (a, n), h)
                 for h, (a, n) in enumerate(near_pieces())]
    for h, (codes, planes, a, n, who, waits, pick, after, part) in enumerate(parts):
        for sem, val in waits:
            g.tensor.wait_ge(sem, val)
        if h >= 2:
            g.tensor.wait_ge(S["cast%d" % (h - 2)], 4)
        for b in range(4):
            if h == 0:
                g.tensor.wait_ge(S["sq%d" % b], 1)
            bank = 512 * (4 * (h % 2) + b)
            out = T.ps[:, bank:bank + n]
            done = S["mm%d" % (4 * h + b)]
            g.tensor.matmul_mx(out, T.sc[:, 128 * b:128 * b + 128], T.ss[:, 128 * b:128 * b + 128],
                               codes[:, a:a + n], planes[:, a:a + n], True, True).then_inc(done, 1)
            to = T.h[:, 4 * a + b:4 * (a + n):4]
            if b % 2 == 1:
                g.vector.wait_ge(done, 1)
                g.vector.tensor_scalar(to, out, SCALE, None, AluOpType.mult).then_inc(S["cast%d" % h], 1)
            else:
                g.scalar.wait_ge(done, 1)
                g.scalar.activation(to, out, ActivationFunctionType.Copy, scale=SCALE).then_inc(S["cast%d" % h], 1)
        g.vector.wait_ge(S["cast%d" % h], 4)
        g.vector.quantize_mx(T.nk[:, a:a + n], T.np[:, a:a + n], T.h[:, 4 * a:4 * (a + n)]).then_inc(S["qz%d" % h], 1)
        o = own[who]
        slot = producers(T, o).index(who)
        sem = S["arr%d_%d" % (slot, part)]
        to = 512 * slot
        g.wait_ge(S["qz%d" % h], 1)
        write(T.cores[o], T.mk[:, to + a:to + a + n].bitcast(dt.uint8), T.nk[:, a:a + n].bitcast(dt.uint8), sem, pick)
        if after:
            d, m = after
            write(T.cores[o], T.mp[:, to + d:to + d + m], T.np[:, d:d + m], sem, pick)
    g.wait_ge(S.sent, sent[0])


def consume(g, core, T, topo, rank):
    S = T.sem
    g.sync.dma_start(T.qt[:], T.q[:, 0:512]).then_inc(S.ldq, 16)
    g.scalar.dma_start(T.kp[:], T.ks[:, 0:W]).then_inc(S.ldp, 16)
    g.sync.dma_start(T.kk[:].bitcast(dt.uint8), T.kc[:, 0:4 * W]).then_inc(S.ldo, 16)
    g.vector.wait_ge(S.ldq, 16)
    g.vector.quantize_mx(T.qk[:], T.qp[:], T.qt[:]).then_inc(S.qq, 1)

    mine = [(T.kk, T.kp, 0, W, 0, [(S.qq, 1), (S.ldp, 16), (S.ldo, 16)])]
    first, near, second = [], [], []
    for s, p in enumerate(producers(T, rank)):
        if neighbour(T, topo, p) is None:
            for h, (a, n) in enumerate(near_pieces()):
                near.append((T.mk, T.mp, 512 * s + a, n, W + 512 * s + a, [(S["arr%d_%d" % (s, h)], 2 * count(NEAR_E))]))
        else:
            x = swaps(T, topo, p)
            c = W - x
            first.append((T.mk, T.mp, 512 * s, c, W + 512 * s, [(S["arr%d_0" % s], 3 * count(KEPT_E))]))
            second.append((T.mk, T.mp, 512 * s + c, x, W + 512 * s + c, [(S["arr%d_1" % s], 2 * count(SWAP_E))]))
    first.sort(key=lambda e: e[3])
    second.sort(key=lambda e: e[3])
    chunks = mine + near + first + second
    n_sync = n_act = 0
    for i, (codes, planes, a, n, d, waits) in enumerate(chunks):
        for sem, val in waits:
            g.tensor.wait_ge(sem, val)
        if i >= 8:
            g.tensor.wait_ge(S["cp%d" % (i - 8)], 1)
        bank = 512 * (i % 8)
        out = T.ps[:, bank:bank + n]
        g.tensor.matmul_mx(out, T.qk[:], T.qp[:], codes[:, a:a + n], planes[:, a:a + n], True, True).then_inc(S["mm%d" % i], 1)
        done = S["cp%d" % i]
        if (len(chunks) - i) % 2 == 1:
            g.vector.wait_ge(S["mm%d" % i], 1)
            g.vector.tensor_copy(T.yo[:, d:d + n], out).then_inc(done, 1)
            g.sync.wait_ge(done, 1)
            g.sync.dma_start(T.y[:, d:d + n], T.yo[:, d:d + n]).then_inc(S.outs, 16)
            n_sync += 16
        else:
            g.scalar.wait_ge(S["mm%d" % i], 1)
            g.scalar.activation(T.yo[:, d:d + n], out, ActivationFunctionType.Copy).then_inc(done, 1)
            g.scalar.wait_ge(done, 1)
            g.scalar.dma_start(T.y[:, d:d + n], T.yo[:, d:d + n]).then_inc(S.outa, 16)
            n_act += 16
    g.sync.wait_ge(S.outs, n_sync)
    g.scalar.wait_ge(S.outa, n_act)


def rank_program(g, core, T, topo):
    rank = T.rank_of(core)
    if rank is None:
        return
    if T.tables["OWN"][rank] == rank:
        consume(g, core, T, topo, rank)
    else:
        produce(g, core, T, topo, rank)
